import numpy as np
import ml_dtypes


def mxq(x, axis, fmt="e4m3"):
    dtype, down = {"e4m3": (ml_dtypes.float8_e4m3fn, 7), "e5m2": (ml_dtypes.float8_e5m2, 14)}[fmt]
    v = np.moveaxis(np.asarray(x, np.float32).astype(ml_dtypes.bfloat16).astype(np.float64), axis, -1)
    blocks = v.reshape(v.shape[:-1] + (-1, 32))
    amax = np.abs(blocks).max(-1, keepdims=True)
    byte = np.maximum(np.where(amax > 0, np.frexp(amax)[1] - 1 + 127, 0) - down, 1)
    scale = np.exp2(byte - 127.0)
    codes = (blocks / scale).astype(np.float32).astype(dtype).astype(np.float64)
    return np.moveaxis((codes * scale).reshape(v.shape), -1, axis)


WIDE = False


def mx_kscale(k):
    if not WIDE:
        return np.ones(k)
    levels = np.array([30, -30])
    if k % 512:
        return np.exp2(np.random.permutation(np.resize(levels, k // 32))).repeat(32)
    a = np.empty((k // 512, 16))
    for p in range(k // 512):
        a[p, :8] = np.random.permutation(np.resize(levels, 8))
        for g in range(8):
            far = levels[np.abs(levels - a[p, g]) >= 10]
            a[p, g + 8] = far[np.random.randint(len(far))]
    return np.exp2(a.ravel()).repeat(32)


BF16 = ml_dtypes.bfloat16


def bf(x):
    return np.asarray(x, np.float32).astype(BF16)


def f64(x):
    return np.asarray(x).astype(np.float64)


E2M1 = np.array([0.0, 0.5, 1.0, 1.5, 2.0, 3.0, 4.0, 6.0, -0.0, -0.5, -1.0, -1.5, -2.0, -3.0, -4.0, -6.0])


def pack_weight(w, fmt):
    k, n = w.shape
    w = f64(bf(w)).reshape(k // 32, 32, n)
    amax = np.abs(w).max(1)
    if fmt in ("e4m3", "e5m2"):
        byte = np.frexp(amax)[1] - 1 + 127 - (7 if fmt == "e4m3" else 14)
    else:
        mant, ex = np.frexp(amax / 6.0)
        byte = np.where(mant > 0.5, ex, ex - 1) + 127
    byte = np.clip(np.where(amax > 0, byte, 1), 1, 254)
    scaled = (w * np.exp2(127.0 - byte)[:, None, :]).reshape(k, n).astype(np.float32)
    by_word = np.ascontiguousarray(scaled.reshape(k // 512, 128, 4, n).transpose(0, 1, 3, 2))
    if fmt in ("e4m3", "e5m2"):
        words = by_word.astype(ml_dtypes.float8_e4m3fn if fmt == "e4m3" else ml_dtypes.float8_e5m2).view(np.uint8)
    else:
        c = by_word.astype(ml_dtypes.float4_e2m1fn).view(np.uint8) & 0xF
        words = c[..., 0::2] | (c[..., 1::2] << 4)
    return np.ascontiguousarray(words), np.ascontiguousarray(byte.astype(np.uint8).reshape(k // 512, 16, n))


def unpack_weight(words, scales, fmt):
    g, p, n, _ = words.shape
    if fmt in ("e4m3", "e5m2"):
        vals = np.ascontiguousarray(words).view(ml_dtypes.float8_e4m3fn if fmt == "e4m3" else ml_dtypes.float8_e5m2).astype(np.float64)
    else:
        nib = np.empty((g, p, n, 4), np.uint8)
        nib[..., 0::2] = words & 0xF
        nib[..., 1::2] = words >> 4
        vals = E2M1[nib]
    vals = vals * np.repeat(np.exp2(scales.astype(np.float64) - 127.0), 8, axis=1)[..., None]
    return vals.transpose(0, 1, 3, 2).reshape(g * 512, n)


V, B, H = 2048, 1536, 1536


def setup_inputs():
    s = mx_kscale(V)
    G = np.random.standard_normal((V, B)) * np.exp(0.5 * np.random.standard_normal((V, B)))
    g_words, g_scales = pack_weight(G * s[:, None], "e5m2")
    w = np.random.standard_normal((V, H)) / np.sqrt(V) / s[:, None]
    h = 1.0 / (1.0 + np.exp(-np.random.standard_normal((B, H))))
    beta = 0.25 + 0.25 * np.abs(np.random.standard_normal(H))
    return {"g_words": g_words,
            "g_scales": g_scales,
            "w": bf(w),
            "h": bf(h),
            "beta": bf(beta)}


def reference(g_words, g_scales, w, h, beta):
    G = unpack_weight(g_words, g_scales, "e5m2")
    back = G.T @ mxq(f64(w), 0, "e4m3")
    a = f64(h)
    return (back + f64(beta)) * (a * (1.0 - a))

@@ -1,0 +1,346 @@
+from contextlib import ExitStack
+
+import concourse.mybir as mybir
+from concourse.masks import make_identity
+
+V, B, H = 2048, 1536, 1536
+FLOPS = 2 * V * B * H
+
+F32 = mybir.dt.float32
+BF16 = mybir.dt.bfloat16
+U32 = mybir.dt.uint32
+I32 = mybir.dt.int32
+U8 = mybir.dt.uint8
+E4M3X4 = mybir.dt.float8_e4m3fn_x4
+E5M2X4 = mybir.dt.float8_e5m2_x4
+ALU = mybir.AluOpType
+ACT = mybir.ActivationFunctionType
+
+P = 128
+PACK = 4
+PASSES = V // (P * PACK)
+BLK = 512
+SUB = BLK // P
+
+ORDER = [(0, 0), (0, 1), (1, 0), (1, 1), (0, 2), (1, 2), (2, 0), (2, 1), (2, 2)]
+TURNED = (0, 1, 2, 3, 4, 5, 6, 7)
+POOL_FACTOR = {**{(k, 3): "s" for k in range(2, 8)}, **{(8, e): "s" for e in range(4)}}
+COPY = {0: "vsvs", 1: "svsv", 2: "ssss"}
+FACTOR_AT = {}
+EXTRA = {
+    "head": [("il", 0, 0), ("cols",), ("q", 0, 0), ("il", 0, 1), ("il", 0, 2), ("q", 0, 1), ("il", 0, 3), ("q", 0, 2), ("cols2",), ("q", 0, 3)],
+    (0, 1): [("f", 0, 0), ("f", 0, 1), ("f", 0, 2), ("f", 0, 3), ("il", 1, 0), ("il", 1, 1), ("il", 1, 2)],
+    (1, 0): [("il", 1, 3), ("q", 1, 0), ("q", 1, 1), ("f", 1, 0), ("f", 1, 1)],
+    (1, 1, "b"): [("q", 1, 2), ("q", 1, 3)],
+    (1, 1): [("f", 1, 2), ("f", 1, 3), ("load", 1)],
+    (2, 0): [("f", 2, 0), ("f", 2, 1), ("f", 2, 3)],
+    (2, 1): [("f", 2, 2)],
+    (3, 0): [("f", 3, 0), ("f", 3, 1), ("f", 3, 3), ("il", 2, 0)],
+    (3, 1): [("f", 3, 2), ("spread", 2), ("il", 2, 1)],
+    (4, 0): [("f", 4, 0), ("f", 4, 1), ("f", 4, 3), ("q", 2, 0), ("il", 2, 2)],
+    (4, 1): [("f", 4, 2), ("q", 2, 1), ("il", 2, 3)],
+    (5, 0): [("f", 5, 0), ("f", 5, 1), ("f", 5, 3), ("q", 2, 2), ("q", 2, 3)],
+    (5, 1): [("f", 5, 2), ("f", 8, 0)],
+    (6, 0): [("f", 6, 0), ("f", 6, 1), ("f", 6, 3)],
+    (6, 1): [("f", 6, 2), ("f", 8, 1)],
+    (7, 0): [("f", 7, 0), ("f", 7, 1), ("f", 7, 3), ("f", 8, 2)],
+    (7, 1): [("f", 7, 2), ("f", 8, 3)],
+}
+LOADS = {
+    0: [("w", 0, 0), ("w", 0, 1), ("s",), ("w", 0, 2), ("w", 0, 3), ("g", 0), ("h", 0, 0, 1), ("g", 1), ("w", 1, 0), ("w", 1, 1), ("w", 1, 2), ("w", 1, 3), ("h", 1, 0, 1), ("h", 0, 1, 3), ("h", 1, 1, 3)],
+    1: [("g", 2), ("h", 2, 0, 3), ("w", 2, 0), ("w", 2, 1), ("w", 2, 2), ("w", 2, 3)],
+}
+STORE_Q = "ggggggggf"
+
+
+def tile_tied_autoencoder_hidden_delta_e1_kernel(tc, g_words, g_scales, w, h, beta, out):
+    nc = tc.nc
+    with ExitStack() as ctx:
+        keep = ctx.enter_context(tc.tile_pool(name="keep", bufs=1))
+        work = ctx.enter_context(tc.tile_pool(name="work", bufs=2))
+        psum = ctx.enter_context(tc.psum_pool(name="psum", bufs=4))
+        ctx.enter_context(tc.manual_schedule())
+
+        words_hbm = g_words.rearrange("g p n t -> p g (n t)")
+
+        beta_rows = keep.tile([P, P], BF16, name="beta_rows")
+        nc.vector.memset(beta_rows[:], 0.0)
+        gs = keep.tile([P, PASSES, B], U8, name="gs", align_bytes=64)
+        nc.vector.memset(gs[:].rearrange("p g n -> p (g n)").bitcast(I32), 0)
+        nc.scalar.dma_start(out=beta_rows[0 : H // P, :], in_=beta.rearrange("(c p) -> c p", p=P))
+        ident = keep.tile([P, P], F32, name="ident")
+        make_identity(nc, ident[:])
+
+        raw = {}
+        gw = {}
+        hs = {}
+
+        def load_w(n, g):
+            t = work.tile([P, PACK, BLK], BF16, name="wraw", bufs=9)
+            nc.sync.dma_start(
+                out=t[:],
+                in_=w[512 * g : 512 * (g + 1), BLK * n : BLK * (n + 1)].rearrange("(p j) c -> p j c", j=PACK),
+            )
+            raw[n, g] = t
+
+        def load_s():
+            for q in range(4):
+                nc.sync.dma_start(
+                    out=gs[32 * q : 32 * q + 4, :, :].bitcast(I32),
+                    in_=g_scales[:, 4 * q : 4 * q + 4, :].rearrange("g q n -> q g n").bitcast(I32),
+                )
+
+        def load_g(c):
+            t = keep.tile([P, PASSES, BLK], U32, name="gw%d" % c, align_bytes=64)
+            step = 2 if c == 0 else PASSES
+            for g in range(0, PASSES, step):
+                nc.sync.dma_start(
+                    out=t[:, g : g + step, :].bitcast(I32),
+                    in_=words_hbm[:, g : g + step, 4 * BLK * c : 4 * BLK * (c + 1)].bitcast(I32),
+                )
+            gw[c] = t
+
+        def load_h(c, n0, n1):
+            t = keep.tile([P, SUB, BLK * (n1 - n0)], BF16, name="h%d_%d" % (c, n0))
+            nc.sync.dma_start(
+                out=t[:],
+                in_=h[BLK * c : BLK * (c + 1), BLK * n0 : BLK * n1].rearrange("(s p) n -> p s n", p=P),
+            )
+            for n in range(n0, n1):
+                hs[c, n] = t[:, :, BLK * (n - n0) : BLK * (n - n0 + 1)]
+
+        def load(spec):
+            kind = spec[0]
+            if kind == "w":
+                load_w(spec[1], spec[2])
+            elif kind == "s":
+                load_s()
+            elif kind == "g":
+                load_g(spec[1])
+            else:
+                load_h(spec[1], spec[2], spec[3])
+
+        for spec in LOADS[0]:
+            load(spec)
+
+        wc = {}
+        ws = {}
+        for n in range(3):
+            wc[n] = keep.tile([P, PASSES, BLK], U32, name="wc%d" % n, align_bytes=64)
+            ws[n] = keep.tile([P, PASSES, BLK], U8, name="ws%d" % n, align_bytes=64)
+        il = {}
+
+        def interleave(n, g):
+            t = work.tile([P, BLK, PACK], BF16, name="il", bufs=4, align_bytes=64)
+            halves = 2 if COPY[n][g] == "s2" else 1
+            wd = BLK // halves
+            for i in range(halves):
+                o = t[:, wd * i : wd * (i + 1), :]
+                x = raw[n, g][:, :, wd * i : wd * (i + 1)].rearrange("p j w -> p w j")
+                if COPY[n][g] == "v":
+                    nc.vector.tensor_copy(out=o, in_=x)
+                elif COPY[n][g] == "g":
+                    nc.gpsimd.tensor_scalar(out=o, in0=x, scalar1=1.0, scalar2=0.0, op0=ALU.mult, op1=ALU.add)
+                else:
+                    nc.scalar.copy(out=o, in_=x)
+            il[n, g] = t
+
+        def quantise(n, g):
+            nc.vector.quantize_mx(
+                out=wc[n][:, g, :].bitcast(E4M3X4),
+                scales=ws[n][:, g, :],
+                in_=il[n, g][:].rearrange("p w j -> p (w j)"),
+            )
+
+        beta_col = keep.tile([P, H // P], F32, name="beta_col")
+        beta_all = {}
+
+        def columns_beta():
+            beta_f32 = keep.tile([P, P], F32, name="beta_f32")
+            nc.vector.tensor_copy(out=beta_f32[:], in_=beta_rows[:])
+            bank = psum.tile([P, BLK], F32, name="turn")
+            nc.tensor.transpose(bank[:, 0:P], beta_f32[:], ident[:])
+            banks["beta"] = bank
+
+        def copy_beta():
+            nc.scalar.copy(out=beta_col[:], in_=banks["beta"][:, 0 : H // P])
+
+        banks = {}
+
+        def spread_beta(n):
+            b = psum.tile([P, BLK], F32, name="turn")
+            for s in range(SUB):
+                k = SUB * n + s
+                nc.tensor.transpose(b[:, P * s : P * (s + 1)], beta_col[:, k : k + 1].to_broadcast([P, P]), ident[:])
+            t = keep.tile([P, BLK], F32, name="beta_all%d" % n)
+            nc.scalar.copy(out=t[:], in_=b[:])
+            beta_all[n] = t
+
+        acc = {}
+        turned = {}
+        fac = {}
+        res = {}
+
+        def one_pass(k, s, g):
+            n, c = ORDER[k]
+            bank = acc[k, s]
+            cols = slice(P * s, P * (s + 1))
+            if k in TURNED:
+                nc.tensor.matmul_mx(
+                    out=bank[:],
+                    lhsT=wc[n][:, g, cols].bitcast(E4M3X4),
+                    lhsT_scale=ws[n][:, g, cols],
+                    rhs=gw[c][:, g, :].bitcast(E5M2X4),
+                    rhs_scale=gs[:, g, BLK * c : BLK * (c + 1)],
+                    start=(g == 0),
+                    stop=(g == PASSES - 1),
+                )
+            else:
+                nc.tensor.matmul_mx(
+                    out=bank[:],
+                    lhsT=gw[c][:, g, cols].bitcast(E5M2X4),
+                    lhsT_scale=gs[:, g, BLK * c + P * s : BLK * c + P * (s + 1)],
+                    rhs=wc[n][:, g, :].bitcast(E4M3X4),
+                    rhs_scale=ws[n][:, g, :],
+                    start=(g == 0),
+                    stop=(g == PASSES - 1),
+                )
+
+        def multiply(k, half):
+            for s in (2 * half, 2 * half + 1):
+                acc[k, s] = psum.tile([P, BLK], F32, name="acc")
+                for g in range(PASSES):
+                    one_pass(k, s, g)
+
+        def evacuate(k, half):
+            n, c = ORDER[k]
+            if k in TURNED:
+                for s in (2 * half, 2 * half + 1):
+                    t = work.tile([P, BLK], F32, name="sum_t", bufs=6)
+                    col = SUB * n + s
+                    nc.scalar.activation(out=t[:], in_=acc[k, s][:], func=ACT.Identity, bias=beta_col[:, col : col + 1])
+                    turned[k, s] = t
+
+        def turn(k, half):
+            if k in TURNED:
+                for e in (2 * half, 2 * half + 1):
+                    b = psum.tile([P, BLK], F32, name="turn")
+                    for s in range(SUB):
+                        nc.tensor.transpose(b[:, P * s : P * (s + 1)], turned[k, s][:, P * e : P * (e + 1)], ident[:])
+                    acc[k, "t", e] = b
+
+        def factor(k, e):
+            n, c = ORDER[k]
+            if k not in fac:
+                fac[k] = {}
+            f = work.tile([P, BLK], F32, name="fac", bufs=12)
+            x = hs[c, n][:, e, :]
+            if (k, e) in POOL_FACTOR:
+                y = work.tile([P, BLK], F32, name="hm1", bufs=2)
+                if POOL_FACTOR[k, e] == "s":
+                    nc.scalar.activation(out=y[:], in_=x, func=ACT.Copy, bias=-1.0)
+                else:
+                    nc.gpsimd.tensor_scalar(out=y[:], in0=x, scalar1=1.0, scalar2=-1.0, op0=ALU.mult, op1=ALU.add)
+                nc.gpsimd.tensor_tensor(out=f[:], in0=y[:], in1=x, op=ALU.mult)
+            else:
+                nc.vector.scalar_tensor_tensor(out=f[:], in0=x, scalar=1.0, in1=x, op0=ALU.subtract, op1=ALU.mult)
+            fac[k][e] = f
+
+        def finish(k, half):
+            n, c = ORDER[k]
+            o = work.tile([P, 2, BLK], F32, name="res", bufs=6)
+            res[k, half] = o
+            pair = (2 * half, 2 * half + 1)
+            src = {}
+            for e in pair:
+                if k in TURNED:
+                    src[e] = acc[k, "t", e]
+                else:
+                    t = work.tile([P, BLK], F32, name="sum_g", bufs=4)
+                    nc.vector.tensor_tensor(out=t[:], in0=acc[k, e][:], in1=beta_all[n][:], op=ALU.add)
+                    src[e] = t
+            for e in pair:
+                nc.vector.scalar_tensor_tensor(
+                    out=o[:, e - 2 * half, :], in0=src[e][:], scalar=-1.0, in1=fac[k][e][:], op0=ALU.mult, op1=ALU.mult,
+                )
+            rows = out[BLK * c : BLK * (c + 1), BLK * n : BLK * (n + 1)].rearrange("(s p) n -> p s n", p=P)
+            if STORE_Q[k] == "g":
+                nc.gpsimd.dma_start(out=rows[:, 2 * half : 2 * half + 2, :], in_=o[:])
+            elif STORE_Q[k] == "s":
+                nc.sync.dma_start(out=rows[:, 2 * half : 2 * half + 2, :], in_=o[:])
+            else:
+                for e in pair:
+                    nc.sync.dma_start(out=rows[:, e, :], in_=o[:, e - 2 * half, :])
+
+        def do(tasks):
+            for t in tasks:
+                if t[0] == "il":
+                    interleave(t[1], t[2])
+                elif t[0] == "q":
+                    quantise(t[1], t[2])
+                elif t[0] == "f":
+                    factor(t[1], t[2])
+                elif t[0] == "spread":
+                    spread_beta(t[1])
+                elif t[0] == "cols":
+                    columns_beta()
+                elif t[0] == "cols2":
+                    copy_beta()
+                elif t[0] == "load":
+                    for spec in LOADS[t[1]]:
+                        load(spec)
+
+        do(EXTRA["head"])
+        for s in range(SUB):
+            acc[0, s] = psum.tile([P, BLK], F32, name="acc")
+        for g in range(PASSES):
+            for s in range(SUB):
+                one_pass(0, s, g)
+        evacuate(0, 0)
+        evacuate(0, 1)
+        do(EXTRA[0, 1])
+        last = len(ORDER) - 1
+        for k in range(1, last):
+            for half in range(2):
+                do(EXTRA.get((k, half, "a"), []))
+                multiply(k, half)
+                if k - 1 in TURNED:
+                    turn(k - 1, half)
+                evacuate(k, half)
+                do(EXTRA.get((k, half, "b"), []))
+                if k - 1 in TURNED:
+                    finish(k - 1, half)
+                if k not in TURNED:
+                    finish(k, half)
+                do(EXTRA.get((k, half), []))
+        k = last
+        n, c = ORDER[k]
+        rows = out[BLK * c : BLK * (c + 1), BLK * n : BLK * (n + 1)].rearrange("(s p) n -> p s n", p=P)
+        sums = {}
+
+        def add_beta(s):
+            sums[s] = work.tile([P, BLK], F32, name="sum_g", bufs=4)
+            nc.vector.tensor_tensor(out=sums[s][:], in0=acc[k, s][:], in1=beta_all[n][:], op=ALU.add)
+
+        def scale(s):
+            o = work.tile([P, 2, BLK], F32, name="res", bufs=6)
+            nc.vector.scalar_tensor_tensor(
+                out=o[:, 0, :], in0=sums[s][:], scalar=-1.0, in1=fac[k][s][:], op0=ALU.mult, op1=ALU.mult,
+            )
+            nc.sync.dma_start(out=rows[:, s, :], in_=o[:, 0, :])
+
+        for s in range(SUB):
+            acc[k, s] = psum.tile([P, BLK], F32, name="acc")
+            for g in range(PASSES):
+                one_pass(k, s, g)
+            if s == 0:
+                turn(k - 1, 0)
+                turn(k - 1, 1)
+                finish(k - 1, 0)
+            if s == 1:
+                finish(k - 1, 1)
+                add_beta(0)
+            if s > 0:
+                add_beta(s)
+                scale(s - 1)
+        scale(SUB - 1)

@@ -24,15 +24,15 @@ SUB = BLK // P
 
 ORDER = [(0, 0), (0, 1), (1, 0), (1, 1), (0, 2), (1, 2), (2, 0), (2, 1), (2, 2)]
 TURNED = (0, 1, 2, 3, 4, 5, 6, 7)
-POOL_FACTOR = {**{(k, 3): "s" for k in range(2, 8)}, **{(8, e): "s" for e in range(4)}}
+POOL_FACTOR = {}
 COPY = {0: "vsvs", 1: "svsv", 2: "ssss"}
 FACTOR_AT = {}
 EXTRA = {
     "head": [("il", 0, 0), ("cols",), ("q", 0, 0), ("il", 0, 1), ("il", 0, 2), ("q", 0, 1), ("il", 0, 3), ("q", 0, 2), ("cols2",), ("q", 0, 3)],
-    (0, 1): [("f", 0, 0), ("f", 0, 1), ("f", 0, 2), ("f", 0, 3), ("il", 1, 0), ("il", 1, 1), ("il", 1, 2)],
+    (0, 1): [("load", 1), ("f", 0, 0), ("f", 0, 1), ("f", 0, 2), ("f", 0, 3), ("il", 1, 0), ("il", 1, 1), ("il", 1, 2)],
     (1, 0): [("il", 1, 3), ("q", 1, 0), ("q", 1, 1), ("f", 1, 0), ("f", 1, 1)],
     (1, 1, "b"): [("q", 1, 2), ("q", 1, 3)],
-    (1, 1): [("f", 1, 2), ("f", 1, 3), ("load", 1)],
+    (1, 1): [("f", 1, 2), ("f", 1, 3)],
     (2, 0): [("f", 2, 0), ("f", 2, 1), ("f", 2, 3)],
     (2, 1): [("f", 2, 2)],
     (3, 0): [("f", 3, 0), ("f", 3, 1), ("f", 3, 3), ("il", 2, 0)],
@@ -50,7 +50,7 @@ LOADS = {
     0: [("w", 0, 0), ("w", 0, 1), ("s",), ("w", 0, 2), ("w", 0, 3), ("g", 0), ("h", 0, 0, 1), ("g", 1), ("w", 1, 0), ("w", 1, 1), ("w", 1, 2), ("w", 1, 3), ("h", 1, 0, 1), ("h", 0, 1, 3), ("h", 1, 1, 3)],
     1: [("g", 2), ("h", 2, 0, 3), ("w", 2, 0), ("w", 2, 1), ("w", 2, 2), ("w", 2, 3)],
 }
-STORE_Q = "ggggggggf"
+STORE_Q = "sssssssss"
 
 
 def tile_tied_autoencoder_hidden_delta_e1_kernel(tc, g_words, g_scales, w, h, beta, out):
@@ -248,7 +248,7 @@ def tile_tied_autoencoder_hidden_delta_e1_kernel(tc, g_words, g_scales, w, h, be
 
         def finish(k, half):
             n, c = ORDER[k]
-            o = work.tile([P, 2, BLK], F32, name="res", bufs=6)
+            o = work.tile([P, 2, BLK], F32, name="res", bufs=8)
             res[k, half] = o
             pair = (2 * half, 2 * half + 1)
             src = {}
@@ -304,8 +304,9 @@ def tile_tied_autoencoder_hidden_delta_e1_kernel(tc, g_words, g_scales, w, h, be
             for half in range(2):
                 do(EXTRA.get((k, half, "a"), []))
                 multiply(k, half)
-                if k - 1 in TURNED:
-                    turn(k - 1, half)
+                if k - 1 in TURNED and half == 0:
+                    turn(k - 1, 0)
+                    turn(k - 1, 1)
                 evacuate(k, half)
                 do(EXTRA.get((k, half, "b"), []))
                 if k - 1 in TURNED:
@@ -323,7 +324,7 @@ def tile_tied_autoencoder_hidden_delta_e1_kernel(tc, g_words, g_scales, w, h, be
             nc.vector.tensor_tensor(out=sums[s][:], in0=acc[k, s][:], in1=beta_all[n][:], op=ALU.add)
 
         def scale(s):
-            o = work.tile([P, 2, BLK], F32, name="res", bufs=6)
+            o = work.tile([P, 2, BLK], F32, name="res", bufs=8)
             nc.vector.scalar_tensor_tensor(
                 out=o[:, 0, :], in0=sums[s][:], scalar=-1.0, in1=fac[k][s][:], op0=ALU.mult, op1=ALU.mult,
             )

@@ -22,34 +22,13 @@ PASSES = V // (P * PACK)
 BLK = 512
 SUB = BLK // P
 
-ORDER = [(0, 0), (0, 1), (1, 0), (1, 1), (0, 2), (1, 2), (2, 0), (2, 1), (2, 2)]
+ORDER = [(n, c) for n in range(3) for c in range(3)]
 TURNED = (0, 1, 2, 3, 4, 5, 6, 7)
 POOL_FACTOR = {}
-COPY = {0: "vsvs", 1: "svsv", 2: "ssss"}
+COPY = {0: 'vsvv', 1: 'vsss', 2: 'ssss'}
 FACTOR_AT = {}
-EXTRA = {
-    "head": [("il", 0, 0), ("cols",), ("q", 0, 0), ("il", 0, 1), ("il", 0, 2), ("q", 0, 1), ("il", 0, 3), ("q", 0, 2), ("cols2",), ("q", 0, 3)],
-    (0, 1): [("load", 1), ("f", 0, 0), ("f", 0, 1), ("f", 0, 2), ("f", 0, 3), ("il", 1, 0), ("il", 1, 1), ("il", 1, 2)],
-    (1, 0): [("il", 1, 3), ("q", 1, 0), ("q", 1, 1), ("f", 1, 0), ("f", 1, 1)],
-    (1, 1, "b"): [("q", 1, 2), ("q", 1, 3)],
-    (1, 1): [("f", 1, 2), ("f", 1, 3)],
-    (2, 0): [("f", 2, 0), ("f", 2, 1), ("f", 2, 3)],
-    (2, 1): [("f", 2, 2)],
-    (3, 0): [("f", 3, 0), ("f", 3, 1), ("f", 3, 3), ("il", 2, 0)],
-    (3, 1): [("f", 3, 2), ("spread", 2), ("il", 2, 1)],
-    (4, 0): [("f", 4, 0), ("f", 4, 1), ("f", 4, 3), ("q", 2, 0), ("il", 2, 2)],
-    (4, 1): [("f", 4, 2), ("q", 2, 1), ("il", 2, 3)],
-    (5, 0): [("f", 5, 0), ("f", 5, 1), ("f", 5, 3), ("q", 2, 2), ("q", 2, 3)],
-    (5, 1): [("f", 5, 2), ("f", 8, 0)],
-    (6, 0): [("f", 6, 0), ("f", 6, 1), ("f", 6, 3)],
-    (6, 1): [("f", 6, 2), ("f", 8, 1)],
-    (7, 0): [("f", 7, 0), ("f", 7, 1), ("f", 7, 3), ("f", 8, 2)],
-    (7, 1): [("f", 7, 2), ("f", 8, 3)],
-}
-LOADS = {
-    0: [("w", 0, 0), ("w", 0, 1), ("s",), ("w", 0, 2), ("w", 0, 3), ("g", 0), ("h", 0, 0, 1), ("g", 1), ("w", 1, 0), ("w", 1, 1), ("w", 1, 2), ("w", 1, 3), ("h", 1, 0, 1), ("h", 0, 1, 3), ("h", 1, 1, 3)],
-    1: [("g", 2), ("h", 2, 0, 3), ("w", 2, 0), ("w", 2, 1), ("w", 2, 2), ("w", 2, 3)],
-}
+EXTRA = {'head': [('load', 1), ('il', 0, 0), ('q', 0, 0), ('il', 0, 2), ('il', 0, 1), ('cols',), ('q', 0, 1), ('il', 0, 3), ('cols2',), ('q', 0, 2), ('q', 0, 3)], (0, 1): [('f', 0, 1), ('f', 0, 2), ('f', 0, 3), ('f', 1, 0), ('f', 0, 0), ('il', 1, 1)], (1, 0): [('il', 1, 3)], (1, 1, 'a'): [('il', 1, 0)], (1, 1, 'b'): [('il', 1, 2)], (2, 0, 'a'): [('f', 2, 3), ('f', 2, 0)], (2, 0, 'b'): [('f', 1, 3), ('f', 1, 1), ('q', 1, 0), ('f', 1, 2)], (2, 0): [('q', 1, 3)], (2, 1, 'a'): [('q', 1, 1)], (2, 1, 'b'): [('q', 1, 2)], (3, 0, 'a'): [('f', 2, 1)], (3, 0, 'b'): [('il', 2, 0), ('f', 4, 0)], (3, 0): [('f', 2, 2)], (3, 1, 'a'): [('f', 4, 2)], (3, 1, 'b'): [('f', 3, 0)], (3, 1): [('il', 2, 2), ('f', 3, 1), ('f', 4, 1)], (4, 0, 'b'): [('il', 2, 1), ('f', 4, 3)], (4, 0): [('spread', 2)], (4, 1, 'a'): [('f', 3, 2), ('f', 3, 3)], (4, 1, 'b'): [('il', 2, 3)], (4, 1): [('q', 2, 0), ('f', 8, 0), ('f', 6, 0)], (5, 0, 'a'): [('q', 2, 2), ('f', 5, 3)], (5, 0, 'b'): [('q', 2, 1)], (5, 0): [('q', 2, 3), ('f', 5, 0)], (5, 1, 'a'): [('f', 8, 3)], (5, 1): [('f', 5, 1), ('f', 6, 1)], (6, 0, 'a'): [('f', 6, 3), ('f', 7, 1)], (6, 0, 'b'): [('f', 8, 1)], (6, 0): [('f', 5, 2)], (6, 1, 'a'): [('f', 8, 2)], (6, 1): [('f', 6, 2)], (7, 1, 'a'): [('f', 7, 0)], (7, 1, 'b'): [('f', 7, 3)], (7, 1): [('f', 7, 2)]}
+LOADS = {0: [('w', 0, 0), ('w', 0, 1), ('w', 0, 2), ('w', 0, 3), ('g', 0, 0, 2), ('s',), ('h', 0, 0, 1), ('g', 0, 2, 4), ('h', 1, 0, 1), ('g', 1, 0, 4), ('w', 1, 1), ('h', 2, 0, 1), ('w', 1, 0), ('w', 1, 3), ('g', 2, 0, 4), ('w', 1, 2)], 1: [('h', 0, 1, 3), ('h', 1, 1, 3), ('w', 2, 0), ('w', 2, 1), ('w', 2, 2), ('h', 2, 1, 3), ('w', 2, 3)]}
 STORE_Q = "sssssssss"
 
 
@@ -90,15 +69,13 @@ def tile_tied_autoencoder_hidden_delta_e1_kernel(tc, g_words, g_scales, w, h, be
                     in_=g_scales[:, 4 * q : 4 * q + 4, :].rearrange("g q n -> q g n").bitcast(I32),
                 )
 
-        def load_g(c):
-            t = keep.tile([P, PASSES, BLK], U32, name="gw%d" % c, align_bytes=64)
-            step = 2 if c == 0 else PASSES
-            for g in range(0, PASSES, step):
-                nc.sync.dma_start(
-                    out=t[:, g : g + step, :].bitcast(I32),
-                    in_=words_hbm[:, g : g + step, 4 * BLK * c : 4 * BLK * (c + 1)].bitcast(I32),
-                )
-            gw[c] = t
+        def load_g(c, g0, g1):
+            if c not in gw:
+                gw[c] = keep.tile([P, PASSES, BLK], U32, name="gw%d" % c, align_bytes=64)
+            nc.sync.dma_start(
+                out=gw[c][:, g0:g1, :].bitcast(I32),
+                in_=words_hbm[:, g0:g1, 4 * BLK * c : 4 * BLK * (c + 1)].bitcast(I32),
+            )
 
         def load_h(c, n0, n1):
             t = keep.tile([P, SUB, BLK * (n1 - n0)], BF16, name="h%d_%d" % (c, n0))
@@ -116,7 +93,7 @@ def tile_tied_autoencoder_hidden_delta_e1_kernel(tc, g_words, g_scales, w, h, be
             elif kind == "s":
                 load_s()
             elif kind == "g":
-                load_g(spec[1])
+                load_g(spec[1], spec[2], spec[3])
             else:
                 load_h(spec[1], spec[2], spec[3])
 

@@ -13,23 +13,27 @@ I32 = mybir.dt.int32
 U8 = mybir.dt.uint8
 E4M3X4 = mybir.dt.float8_e4m3fn_x4
 E5M2X4 = mybir.dt.float8_e5m2_x4
-ALU = mybir.AluOpType
-ACT = mybir.ActivationFunctionType
+ADD, SUB, MULT = mybir.AluOpType.add, mybir.AluOpType.subtract, mybir.AluOpType.mult
+IDENTITY = mybir.ActivationFunctionType.Identity
 
 P = 128
 PACK = 4
-PASSES = V // (P * PACK)
-BLK = 512
-SUB = BLK // P
+K_PASS = P * PACK
+PASSES = V // K_PASS
+BLOCK = 512
+QUARTERS = BLOCK // P
+EX_BLOCKS = B // BLOCK
+HID_BLOCKS = H // BLOCK
 
-ORDER = [(n, c) for n in range(3) for c in range(3)]
-TURNED = (0, 1, 2, 3, 4, 5, 6, 7)
-POOL_FACTOR = {}
-COPY = {0: 'vsvv', 1: 'vsss', 2: 'ssss'}
-FACTOR_AT = {}
-EXTRA = {'head': [('load', 1), ('il', 0, 0), ('q', 0, 0), ('il', 0, 2), ('il', 0, 1), ('cols',), ('q', 0, 1), ('il', 0, 3), ('cols2',), ('q', 0, 2), ('q', 0, 3)], (0, 1): [('f', 0, 1), ('f', 0, 2), ('f', 0, 3), ('f', 1, 0), ('f', 0, 0), ('il', 1, 1)], (1, 0): [('il', 1, 3)], (1, 1, 'a'): [('il', 1, 0)], (1, 1, 'b'): [('il', 1, 2)], (2, 0, 'a'): [('f', 2, 3), ('f', 2, 0)], (2, 0, 'b'): [('f', 1, 3), ('f', 1, 1), ('q', 1, 0), ('f', 1, 2)], (2, 0): [('q', 1, 3)], (2, 1, 'a'): [('q', 1, 1)], (2, 1, 'b'): [('q', 1, 2)], (3, 0, 'a'): [('f', 2, 1)], (3, 0, 'b'): [('il', 2, 0), ('f', 4, 0)], (3, 0): [('f', 2, 2)], (3, 1, 'a'): [('f', 4, 2)], (3, 1, 'b'): [('f', 3, 0)], (3, 1): [('il', 2, 2), ('f', 3, 1), ('f', 4, 1)], (4, 0, 'b'): [('il', 2, 1), ('f', 4, 3)], (4, 0): [('spread', 2)], (4, 1, 'a'): [('f', 3, 2), ('f', 3, 3)], (4, 1, 'b'): [('il', 2, 3)], (4, 1): [('q', 2, 0), ('f', 8, 0), ('f', 6, 0)], (5, 0, 'a'): [('q', 2, 2), ('f', 5, 3)], (5, 0, 'b'): [('q', 2, 1)], (5, 0): [('q', 2, 3), ('f', 5, 0)], (5, 1, 'a'): [('f', 8, 3)], (5, 1): [('f', 5, 1), ('f', 6, 1)], (6, 0, 'a'): [('f', 6, 3), ('f', 7, 1)], (6, 0, 'b'): [('f', 8, 1)], (6, 0): [('f', 5, 2)], (6, 1, 'a'): [('f', 8, 2)], (6, 1): [('f', 6, 2)], (7, 1, 'a'): [('f', 7, 0)], (7, 1, 'b'): [('f', 7, 3)], (7, 1): [('f', 7, 2)]}
-LOADS = {0: [('w', 0, 0), ('w', 0, 1), ('w', 0, 2), ('w', 0, 3), ('g', 0, 0, 2), ('s',), ('h', 0, 0, 1), ('g', 0, 2, 4), ('h', 1, 0, 1), ('g', 1, 0, 4), ('w', 1, 1), ('h', 2, 0, 1), ('w', 1, 0), ('w', 1, 3), ('g', 2, 0, 4), ('w', 1, 2)], 1: [('h', 0, 1, 3), ('h', 1, 1, 3), ('w', 2, 0), ('w', 2, 1), ('w', 2, 2), ('h', 2, 1, 3), ('w', 2, 3)]}
-STORE_Q = "sssssssss"
+STEPS = [(n, c) for n in range(HID_BLOCKS) for c in range(EX_BLOCKS)]
+LAST = len(STEPS) - 1
+
+COPY_ON_VECTOR = {(0, 0), (0, 2), (0, 3), (1, 2)}
+
+COPY_AT = {1: (1, 2, 3, 3), 2: (6, 7, 8, 9)}
+QUANTISE_AT = {1: (4, 4, 5, 5), 2: (10, 10, 11, 11)}
+LAST_FACTORS_AT = (9, 11, 13, 15)
+SPREAD_BETA_AT = 8
 
 
 def tile_tied_autoencoder_hidden_delta_e1_kernel(tc, g_words, g_scales, w, h, beta, out):
@@ -40,285 +44,248 @@ def tile_tied_autoencoder_hidden_delta_e1_kernel(tc, g_words, g_scales, w, h, be
         psum = ctx.enter_context(tc.psum_pool(name="psum", bufs=4))
         ctx.enter_context(tc.manual_schedule())
 
-        words_hbm = g_words.rearrange("g p n t -> p g (n t)")
-
         beta_rows = keep.tile([P, P], BF16, name="beta_rows")
         nc.vector.memset(beta_rows[:], 0.0)
-        gs = keep.tile([P, PASSES, B], U8, name="gs", align_bytes=64)
-        nc.vector.memset(gs[:].rearrange("p g n -> p (g n)").bitcast(I32), 0)
         nc.scalar.dma_start(out=beta_rows[0 : H // P, :], in_=beta.rearrange("(c p) -> c p", p=P))
-        ident = keep.tile([P, P], F32, name="ident")
-        make_identity(nc, ident[:])
 
-        raw = {}
-        gw = {}
-        hs = {}
+        g_scale = keep.tile([P, PASSES, B], U8, name="g_scale", align_bytes=64)
+        nc.vector.memset(g_scale[:].rearrange("p g n -> p (g n)").bitcast(I32), 0)
+
+        identity = keep.tile([P, P], F32, name="identity")
+        make_identity(nc, identity[:])
+
+        w_raw = {}
+        g_code = {}
+        h_view = {}
 
         def load_w(n, g):
-            t = work.tile([P, PACK, BLK], BF16, name="wraw", bufs=9)
-            nc.sync.dma_start(
-                out=t[:],
-                in_=w[512 * g : 512 * (g + 1), BLK * n : BLK * (n + 1)].rearrange("(p j) c -> p j c", j=PACK),
-            )
-            raw[n, g] = t
-
-        def load_s():
-            for q in range(4):
-                nc.sync.dma_start(
-                    out=gs[32 * q : 32 * q + 4, :, :].bitcast(I32),
-                    in_=g_scales[:, 4 * q : 4 * q + 4, :].rearrange("g q n -> q g n").bitcast(I32),
-                )
+            w_raw[n, g] = work.tile([P, PACK, BLOCK], BF16, name="w_raw", bufs=9)
+            rows = w[K_PASS * g : K_PASS * (g + 1), BLOCK * n : BLOCK * (n + 1)]
+            nc.sync.dma_start(out=w_raw[n, g][:], in_=rows.rearrange("(p t) n -> p t n", t=PACK))
 
         def load_g(c, g0, g1):
-            if c not in gw:
-                gw[c] = keep.tile([P, PASSES, BLK], U32, name="gw%d" % c, align_bytes=64)
+            if c not in g_code:
+                g_code[c] = keep.tile([P, PASSES, BLOCK], U32, name="g_code%d" % c, align_bytes=64)
+            words = g_words.rearrange("g p n t -> p g (n t)")
             nc.sync.dma_start(
-                out=gw[c][:, g0:g1, :].bitcast(I32),
-                in_=words_hbm[:, g0:g1, 4 * BLK * c : 4 * BLK * (c + 1)].bitcast(I32),
+                out=g_code[c][:, g0:g1, :].bitcast(I32),
+                in_=words[:, g0:g1, PACK * BLOCK * c : PACK * BLOCK * (c + 1)].bitcast(I32),
             )
+
+        def load_g_scales():
+            for i in range(4):
+                nc.sync.dma_start(
+                    out=g_scale[32 * i : 32 * i + 4, :, :].bitcast(I32),
+                    in_=g_scales[:, 4 * i : 4 * i + 4, :].rearrange("g q n -> q g n").bitcast(I32),
+                )
 
         def load_h(c, n0, n1):
-            t = keep.tile([P, SUB, BLK * (n1 - n0)], BF16, name="h%d_%d" % (c, n0))
-            nc.sync.dma_start(
-                out=t[:],
-                in_=h[BLK * c : BLK * (c + 1), BLK * n0 : BLK * n1].rearrange("(s p) n -> p s n", p=P),
-            )
+            t = keep.tile([P, QUARTERS, BLOCK * (n1 - n0)], BF16, name="h%d_%d" % (c, n0))
+            rows = h[BLOCK * c : BLOCK * (c + 1), BLOCK * n0 : BLOCK * n1]
+            nc.sync.dma_start(out=t[:], in_=rows.rearrange("(e p) n -> p e n", p=P))
             for n in range(n0, n1):
-                hs[c, n] = t[:, :, BLK * (n - n0) : BLK * (n - n0 + 1)]
+                h_view[n, c] = t[:, :, BLOCK * (n - n0) : BLOCK * (n - n0 + 1)]
 
-        def load(spec):
-            kind = spec[0]
-            if kind == "w":
-                load_w(spec[1], spec[2])
-            elif kind == "s":
-                load_s()
-            elif kind == "g":
-                load_g(spec[1], spec[2], spec[3])
-            else:
-                load_h(spec[1], spec[2], spec[3])
+        for g in range(PASSES):
+            load_w(0, g)
+        load_g(0, 0, 2)
+        load_g_scales()
+        load_h(0, 0, 1)
+        load_g(0, 2, 4)
+        load_h(1, 0, 1)
+        load_g(1, 0, 4)
+        load_w(1, 0)
+        load_h(2, 0, 1)
+        load_w(1, 1)
+        load_w(1, 2)
+        load_g(2, 0, 4)
+        load_w(1, 3)
+        load_h(0, 1, 3)
+        load_h(1, 1, 3)
+        load_w(2, 0)
+        load_w(2, 1)
+        load_w(2, 2)
+        load_h(2, 1, 3)
+        load_w(2, 3)
 
-        for spec in LOADS[0]:
-            load(spec)
-
-        wc = {}
-        ws = {}
-        for n in range(3):
-            wc[n] = keep.tile([P, PASSES, BLK], U32, name="wc%d" % n, align_bytes=64)
-            ws[n] = keep.tile([P, PASSES, BLK], U8, name="ws%d" % n, align_bytes=64)
-        il = {}
+        w_code = {}
+        w_scale = {}
+        for n in range(HID_BLOCKS):
+            w_code[n] = keep.tile([P, PASSES, BLOCK], U32, name="w_code%d" % n, align_bytes=64)
+            w_scale[n] = keep.tile([P, PASSES, BLOCK], U8, name="w_scale%d" % n, align_bytes=64)
+        w_grouped = {}
 
         def interleave(n, g):
-            t = work.tile([P, BLK, PACK], BF16, name="il", bufs=4, align_bytes=64)
-            halves = 2 if COPY[n][g] == "s2" else 1
-            wd = BLK // halves
-            for i in range(halves):
-                o = t[:, wd * i : wd * (i + 1), :]
-                x = raw[n, g][:, :, wd * i : wd * (i + 1)].rearrange("p j w -> p w j")
-                if COPY[n][g] == "v":
-                    nc.vector.tensor_copy(out=o, in_=x)
-                elif COPY[n][g] == "g":
-                    nc.gpsimd.tensor_scalar(out=o, in0=x, scalar1=1.0, scalar2=0.0, op0=ALU.mult, op1=ALU.add)
-                else:
-                    nc.scalar.copy(out=o, in_=x)
-            il[n, g] = t
+            w_grouped[n, g] = work.tile([P, BLOCK, PACK], BF16, name="w_grouped", bufs=4, align_bytes=64)
+            copy = nc.vector.tensor_copy if (n, g) in COPY_ON_VECTOR else nc.scalar.copy
+            copy(out=w_grouped[n, g][:], in_=w_raw[n, g][:].rearrange("p t n -> p n t"))
 
         def quantise(n, g):
             nc.vector.quantize_mx(
-                out=wc[n][:, g, :].bitcast(E4M3X4),
-                scales=ws[n][:, g, :],
-                in_=il[n, g][:].rearrange("p w j -> p (w j)"),
+                out=w_code[n][:, g, :].bitcast(E4M3X4),
+                scales=w_scale[n][:, g, :],
+                in_=w_grouped[n, g][:].rearrange("p n t -> p (n t)"),
             )
 
-        beta_col = keep.tile([P, H // P], F32, name="beta_col")
-        beta_all = {}
+        beta_f32 = keep.tile([P, P], F32, name="beta_f32")
+        beta_column = keep.tile([P, H // P], F32, name="beta_column")
+        beta_spread = keep.tile([P, BLOCK], F32, name="beta_spread")
 
-        def columns_beta():
-            beta_f32 = keep.tile([P, P], F32, name="beta_f32")
+        def turn_beta():
             nc.vector.tensor_copy(out=beta_f32[:], in_=beta_rows[:])
-            bank = psum.tile([P, BLK], F32, name="turn")
-            nc.tensor.transpose(bank[:, 0:P], beta_f32[:], ident[:])
-            banks["beta"] = bank
+            bank = psum.tile([P, BLOCK], F32, name="turn")
+            nc.tensor.transpose(bank[:, 0:P], beta_f32[:], identity[:])
+            return bank
 
-        def copy_beta():
-            nc.scalar.copy(out=beta_col[:], in_=banks["beta"][:, 0 : H // P])
-
-        banks = {}
-
-        def spread_beta(n):
-            b = psum.tile([P, BLK], F32, name="turn")
-            for s in range(SUB):
-                k = SUB * n + s
-                nc.tensor.transpose(b[:, P * s : P * (s + 1)], beta_col[:, k : k + 1].to_broadcast([P, P]), ident[:])
-            t = keep.tile([P, BLK], F32, name="beta_all%d" % n)
-            nc.scalar.copy(out=t[:], in_=b[:])
-            beta_all[n] = t
+        def spread_beta():
+            bank = psum.tile([P, BLOCK], F32, name="turn")
+            first = QUARTERS * (HID_BLOCKS - 1)
+            for s in range(QUARTERS):
+                column = beta_column[:, first + s : first + s + 1].to_broadcast([P, P])
+                nc.tensor.transpose(bank[:, P * s : P * (s + 1)], column, identity[:])
+            nc.scalar.copy(out=beta_spread[:], in_=bank[:])
 
         acc = {}
+        sums = {}
         turned = {}
-        fac = {}
-        res = {}
+        factor = {}
+
+        def open_bank(k, s):
+            acc[k, s] = psum.tile([P, BLOCK], F32, name="acc")
 
         def one_pass(k, s, g):
-            n, c = ORDER[k]
-            bank = acc[k, s]
-            cols = slice(P * s, P * (s + 1))
-            if k in TURNED:
-                nc.tensor.matmul_mx(
-                    out=bank[:],
-                    lhsT=wc[n][:, g, cols].bitcast(E4M3X4),
-                    lhsT_scale=ws[n][:, g, cols],
-                    rhs=gw[c][:, g, :].bitcast(E5M2X4),
-                    rhs_scale=gs[:, g, BLK * c : BLK * (c + 1)],
-                    start=(g == 0),
-                    stop=(g == PASSES - 1),
-                )
+            n, c = STEPS[k]
+            quarter = slice(P * s, P * (s + 1))
+            w_side = (w_code[n][:, g, :], w_scale[n][:, g, :])
+            g_side = (g_code[c][:, g, :], g_scale[:, g, BLOCK * c : BLOCK * (c + 1)])
+            if k < LAST:
+                (still, still_scale), still_type = w_side, E4M3X4
+                (moving, moving_scale), moving_type = g_side, E5M2X4
             else:
-                nc.tensor.matmul_mx(
-                    out=bank[:],
-                    lhsT=gw[c][:, g, cols].bitcast(E5M2X4),
-                    lhsT_scale=gs[:, g, BLK * c + P * s : BLK * c + P * (s + 1)],
-                    rhs=wc[n][:, g, :].bitcast(E4M3X4),
-                    rhs_scale=ws[n][:, g, :],
-                    start=(g == 0),
-                    stop=(g == PASSES - 1),
-                )
-
-        def multiply(k, half):
-            for s in (2 * half, 2 * half + 1):
-                acc[k, s] = psum.tile([P, BLK], F32, name="acc")
-                for g in range(PASSES):
-                    one_pass(k, s, g)
-
-        def evacuate(k, half):
-            n, c = ORDER[k]
-            if k in TURNED:
-                for s in (2 * half, 2 * half + 1):
-                    t = work.tile([P, BLK], F32, name="sum_t", bufs=6)
-                    col = SUB * n + s
-                    nc.scalar.activation(out=t[:], in_=acc[k, s][:], func=ACT.Identity, bias=beta_col[:, col : col + 1])
-                    turned[k, s] = t
-
-        def turn(k, half):
-            if k in TURNED:
-                for e in (2 * half, 2 * half + 1):
-                    b = psum.tile([P, BLK], F32, name="turn")
-                    for s in range(SUB):
-                        nc.tensor.transpose(b[:, P * s : P * (s + 1)], turned[k, s][:, P * e : P * (e + 1)], ident[:])
-                    acc[k, "t", e] = b
-
-        def factor(k, e):
-            n, c = ORDER[k]
-            if k not in fac:
-                fac[k] = {}
-            f = work.tile([P, BLK], F32, name="fac", bufs=12)
-            x = hs[c, n][:, e, :]
-            if (k, e) in POOL_FACTOR:
-                y = work.tile([P, BLK], F32, name="hm1", bufs=2)
-                if POOL_FACTOR[k, e] == "s":
-                    nc.scalar.activation(out=y[:], in_=x, func=ACT.Copy, bias=-1.0)
-                else:
-                    nc.gpsimd.tensor_scalar(out=y[:], in0=x, scalar1=1.0, scalar2=-1.0, op0=ALU.mult, op1=ALU.add)
-                nc.gpsimd.tensor_tensor(out=f[:], in0=y[:], in1=x, op=ALU.mult)
-            else:
-                nc.vector.scalar_tensor_tensor(out=f[:], in0=x, scalar=1.0, in1=x, op0=ALU.subtract, op1=ALU.mult)
-            fac[k][e] = f
-
-        def finish(k, half):
-            n, c = ORDER[k]
-            o = work.tile([P, 2, BLK], F32, name="res", bufs=8)
-            res[k, half] = o
-            pair = (2 * half, 2 * half + 1)
-            src = {}
-            for e in pair:
-                if k in TURNED:
-                    src[e] = acc[k, "t", e]
-                else:
-                    t = work.tile([P, BLK], F32, name="sum_g", bufs=4)
-                    nc.vector.tensor_tensor(out=t[:], in0=acc[k, e][:], in1=beta_all[n][:], op=ALU.add)
-                    src[e] = t
-            for e in pair:
-                nc.vector.scalar_tensor_tensor(
-                    out=o[:, e - 2 * half, :], in0=src[e][:], scalar=-1.0, in1=fac[k][e][:], op0=ALU.mult, op1=ALU.mult,
-                )
-            rows = out[BLK * c : BLK * (c + 1), BLK * n : BLK * (n + 1)].rearrange("(s p) n -> p s n", p=P)
-            if STORE_Q[k] == "g":
-                nc.gpsimd.dma_start(out=rows[:, 2 * half : 2 * half + 2, :], in_=o[:])
-            elif STORE_Q[k] == "s":
-                nc.sync.dma_start(out=rows[:, 2 * half : 2 * half + 2, :], in_=o[:])
-            else:
-                for e in pair:
-                    nc.sync.dma_start(out=rows[:, e, :], in_=o[:, e - 2 * half, :])
-
-        def do(tasks):
-            for t in tasks:
-                if t[0] == "il":
-                    interleave(t[1], t[2])
-                elif t[0] == "q":
-                    quantise(t[1], t[2])
-                elif t[0] == "f":
-                    factor(t[1], t[2])
-                elif t[0] == "spread":
-                    spread_beta(t[1])
-                elif t[0] == "cols":
-                    columns_beta()
-                elif t[0] == "cols2":
-                    copy_beta()
-                elif t[0] == "load":
-                    for spec in LOADS[t[1]]:
-                        load(spec)
-
-        do(EXTRA["head"])
-        for s in range(SUB):
-            acc[0, s] = psum.tile([P, BLK], F32, name="acc")
-        for g in range(PASSES):
-            for s in range(SUB):
-                one_pass(0, s, g)
-        evacuate(0, 0)
-        evacuate(0, 1)
-        do(EXTRA[0, 1])
-        last = len(ORDER) - 1
-        for k in range(1, last):
-            for half in range(2):
-                do(EXTRA.get((k, half, "a"), []))
-                multiply(k, half)
-                if k - 1 in TURNED and half == 0:
-                    turn(k - 1, 0)
-                    turn(k - 1, 1)
-                evacuate(k, half)
-                do(EXTRA.get((k, half, "b"), []))
-                if k - 1 in TURNED:
-                    finish(k - 1, half)
-                if k not in TURNED:
-                    finish(k, half)
-                do(EXTRA.get((k, half), []))
-        k = last
-        n, c = ORDER[k]
-        rows = out[BLK * c : BLK * (c + 1), BLK * n : BLK * (n + 1)].rearrange("(s p) n -> p s n", p=P)
-        sums = {}
-
-        def add_beta(s):
-            sums[s] = work.tile([P, BLK], F32, name="sum_g", bufs=4)
-            nc.vector.tensor_tensor(out=sums[s][:], in0=acc[k, s][:], in1=beta_all[n][:], op=ALU.add)
-
-        def scale(s):
-            o = work.tile([P, 2, BLK], F32, name="res", bufs=8)
-            nc.vector.scalar_tensor_tensor(
-                out=o[:, 0, :], in0=sums[s][:], scalar=-1.0, in1=fac[k][s][:], op0=ALU.mult, op1=ALU.mult,
+                (still, still_scale), still_type = g_side, E5M2X4
+                (moving, moving_scale), moving_type = w_side, E4M3X4
+            nc.tensor.matmul_mx(
+                out=acc[k, s][:],
+                lhsT=still[:, quarter].bitcast(still_type),
+                lhsT_scale=still_scale[:, quarter],
+                rhs=moving.bitcast(moving_type),
+                rhs_scale=moving_scale,
+                start=(g == 0),
+                stop=(g == PASSES - 1),
             )
-            nc.sync.dma_start(out=rows[:, s, :], in_=o[:, 0, :])
 
-        for s in range(SUB):
-            acc[k, s] = psum.tile([P, BLK], F32, name="acc")
+        def multiply(k, s):
+            open_bank(k, s)
             for g in range(PASSES):
                 one_pass(k, s, g)
-            if s == 0:
-                turn(k - 1, 0)
-                turn(k - 1, 1)
-                finish(k - 1, 0)
-            if s == 1:
-                finish(k - 1, 1)
-                add_beta(0)
-            if s > 0:
-                add_beta(s)
-                scale(s - 1)
-        scale(SUB - 1)
+
+        def empty_with_beta(k, s):
+            n, c = STEPS[k]
+            sums[k, s] = work.tile([P, BLOCK], F32, name="sums", bufs=6)
+            col = QUARTERS * n + s
+            nc.scalar.activation(
+                out=sums[k, s][:], in_=acc[k, s][:], func=IDENTITY, bias=beta_column[:, col : col + 1]
+            )
+
+        def turn(k):
+            for e in range(QUARTERS):
+                turned[k, e] = psum.tile([P, BLOCK], F32, name="turn")
+                for s in range(QUARTERS):
+                    nc.tensor.transpose(
+                        turned[k, e][:, P * s : P * (s + 1)], sums[k, s][:, P * e : P * (e + 1)], identity[:]
+                    )
+
+        def make_factor(k, e):
+            x = h_view[STEPS[k]][:, e, :]
+            factor[k, e] = work.tile([P, BLOCK], F32, name="factor", bufs=12)
+            nc.vector.scalar_tensor_tensor(out=factor[k, e][:], in0=x, scalar=1.0, in1=x, op0=SUB, op1=MULT)
+
+        def scale_by_factor(out_tile, summed, k, e):
+            nc.vector.scalar_tensor_tensor(
+                out=out_tile, in0=summed[:], scalar=-1.0, in1=factor[k, e][:], op0=MULT, op1=MULT
+            )
+
+        def rows_of(k):
+            n, c = STEPS[k]
+            block = out[BLOCK * c : BLOCK * (c + 1), BLOCK * n : BLOCK * (n + 1)]
+            return block.rearrange("(e p) n -> p e n", p=P)
+
+        def finish(k, half):
+            result = work.tile([P, 2, BLOCK], F32, name="result", bufs=8)
+            for i in range(2):
+                scale_by_factor(result[:, i, :], turned[k, 2 * half + i], k, 2 * half + i)
+            nc.sync.dma_start(out=rows_of(k)[:, 2 * half : 2 * half + 2, :], in_=result[:])
+
+        def side_work(t):
+            for n in COPY_AT:
+                for g in range(PASSES):
+                    if COPY_AT[n][g] == t:
+                        interleave(n, g)
+                for g in range(PASSES):
+                    if QUANTISE_AT[n][g] == t:
+                        quantise(n, g)
+            if t == SPREAD_BETA_AT:
+                spread_beta()
+            k, half = divmod(t, 2)
+            for e in (2 * half, 2 * half + 1):
+                make_factor(k, e)
+            for e in range(QUARTERS):
+                if LAST_FACTORS_AT[e] == t:
+                    make_factor(LAST, e)
+
+        interleave(0, 0)
+        quantise(0, 0)
+        interleave(0, 2)
+        interleave(0, 1)
+        beta_bank = turn_beta()
+        quantise(0, 1)
+        interleave(0, 3)
+        nc.scalar.copy(out=beta_column[:], in_=beta_bank[:, 0 : H // P])
+        quantise(0, 2)
+        quantise(0, 3)
+
+        for s in range(QUARTERS):
+            open_bank(0, s)
+        for g in range(PASSES):
+            for s in range(QUARTERS):
+                one_pass(0, s, g)
+        for s in range(QUARTERS):
+            empty_with_beta(0, s)
+        side_work(0)
+        side_work(1)
+
+        for k in range(1, LAST):
+            for half in range(2):
+                for s in (2 * half, 2 * half + 1):
+                    multiply(k, s)
+                if half == 0:
+                    turn(k - 1)
+                for s in (2 * half, 2 * half + 1):
+                    empty_with_beta(k, s)
+                side_work(2 * k + half)
+                finish(k - 1, half)
+
+        with_beta = {}
+
+        def add_beta(e):
+            with_beta[e] = work.tile([P, BLOCK], F32, name="with_beta", bufs=4)
+            nc.vector.tensor_tensor(out=with_beta[e][:], in0=acc[LAST, e][:], in1=beta_spread[:], op=ADD)
+
+        def finish_last(e):
+            result = work.tile([P, BLOCK], F32, name="result_last", bufs=4)
+            scale_by_factor(result[:], with_beta[e], LAST, e)
+            nc.sync.dma_start(out=rows_of(LAST)[:, e, :], in_=result[:])
+
+        multiply(LAST, 0)
+        turn(LAST - 1)
+        finish(LAST - 1, 0)
+        multiply(LAST, 1)
+        finish(LAST - 1, 1)
+        add_beta(0)
+        add_beta(1)
+        finish_last(0)
+        for e in (2, 3):
+            multiply(LAST, e)
+            add_beta(e)
+            finish_last(e - 1)
+        finish_last(3)

from contextlib import ExitStack

import concourse.mybir as mybir
from concourse.masks import make_identity

V, B, H = 2048, 1536, 1536
FLOPS = 2 * V * B * H

F32 = mybir.dt.float32
BF16 = mybir.dt.bfloat16
U32 = mybir.dt.uint32
I32 = mybir.dt.int32
U8 = mybir.dt.uint8
E4M3X4 = mybir.dt.float8_e4m3fn_x4
E5M2X4 = mybir.dt.float8_e5m2_x4
ADD, SUB, MULT = mybir.AluOpType.add, mybir.AluOpType.subtract, mybir.AluOpType.mult
IDENTITY = mybir.ActivationFunctionType.Identity

P = 128
PACK = 4
K_PASS = P * PACK
PASSES = V // K_PASS
BLOCK = 512
QUARTERS = BLOCK // P
EX_BLOCKS = B // BLOCK
HID_BLOCKS = H // BLOCK

STEPS = [(n, c) for n in range(HID_BLOCKS) for c in range(EX_BLOCKS)]
LAST = len(STEPS) - 1

COPY_ON_VECTOR = {(0, 0), (0, 2), (0, 3), (1, 2)}

COPY_AT = {1: (1, 2, 3, 3), 2: (6, 7, 8, 9)}
QUANTISE_AT = {1: (4, 4, 5, 5), 2: (10, 10, 11, 11)}
LAST_FACTORS_AT = (9, 11, 13, 15)
SPREAD_BETA_AT = 8


def tile_tied_autoencoder_hidden_delta_e1_kernel(tc, g_words, g_scales, w, h, beta, out):
    nc = tc.nc
    with ExitStack() as ctx:
        keep = ctx.enter_context(tc.tile_pool(name="keep", bufs=1))
        work = ctx.enter_context(tc.tile_pool(name="work", bufs=2))
        psum = ctx.enter_context(tc.psum_pool(name="psum", bufs=4))
        ctx.enter_context(tc.manual_schedule())

        beta_rows = keep.tile([P, P], BF16, name="beta_rows")
        nc.vector.memset(beta_rows[:], 0.0)
        nc.scalar.dma_start(out=beta_rows[0 : H // P, :], in_=beta.rearrange("(c p) -> c p", p=P))

        g_scale = keep.tile([P, PASSES, B], U8, name="g_scale", align_bytes=64)
        nc.vector.memset(g_scale[:].rearrange("p g n -> p (g n)").bitcast(I32), 0)

        identity = keep.tile([P, P], F32, name="identity")
        make_identity(nc, identity[:])

        w_raw = {}
        g_code = {}
        h_view = {}

        def load_w(n, g):
            w_raw[n, g] = work.tile([P, PACK, BLOCK], BF16, name="w_raw", bufs=9)
            rows = w[K_PASS * g : K_PASS * (g + 1), BLOCK * n : BLOCK * (n + 1)]
            nc.sync.dma_start(out=w_raw[n, g][:], in_=rows.rearrange("(p t) n -> p t n", t=PACK))

        def load_g(c, g0, g1):
            if c not in g_code:
                g_code[c] = keep.tile([P, PASSES, BLOCK], U32, name="g_code%d" % c, align_bytes=64)
            words = g_words.rearrange("g p n t -> p g (n t)")
            nc.sync.dma_start(
                out=g_code[c][:, g0:g1, :].bitcast(I32),
                in_=words[:, g0:g1, PACK * BLOCK * c : PACK * BLOCK * (c + 1)].bitcast(I32),
            )

        def load_g_scales():
            for i in range(4):
                nc.sync.dma_start(
                    out=g_scale[32 * i : 32 * i + 4, :, :].bitcast(I32),
                    in_=g_scales[:, 4 * i : 4 * i + 4, :].rearrange("g q n -> q g n").bitcast(I32),
                )

        def load_h(c, n0, n1):
            t = keep.tile([P, QUARTERS, BLOCK * (n1 - n0)], BF16, name="h%d_%d" % (c, n0))
            rows = h[BLOCK * c : BLOCK * (c + 1), BLOCK * n0 : BLOCK * n1]
            nc.sync.dma_start(out=t[:], in_=rows.rearrange("(e p) n -> p e n", p=P))
            for n in range(n0, n1):
                h_view[n, c] = t[:, :, BLOCK * (n - n0) : BLOCK * (n - n0 + 1)]

        for g in range(PASSES):
            load_w(0, g)
        load_g(0, 0, 2)
        load_g_scales()
        load_h(0, 0, 1)
        load_g(0, 2, 4)
        load_h(1, 0, 1)
        load_g(1, 0, 4)
        load_w(1, 0)
        load_h(2, 0, 1)
        load_w(1, 1)
        load_w(1, 2)
        load_g(2, 0, 4)
        load_w(1, 3)
        load_h(0, 1, 3)
        load_h(1, 1, 3)
        load_w(2, 0)
        load_w(2, 1)
        load_w(2, 2)
        load_h(2, 1, 3)
        load_w(2, 3)

        w_code = {}
        w_scale = {}
        for n in range(HID_BLOCKS):
            w_code[n] = keep.tile([P, PASSES, BLOCK], U32, name="w_code%d" % n, align_bytes=64)
            w_scale[n] = keep.tile([P, PASSES, BLOCK], U8, name="w_scale%d" % n, align_bytes=64)
        w_grouped = {}

        def interleave(n, g):
            w_grouped[n, g] = work.tile([P, BLOCK, PACK], BF16, name="w_grouped", bufs=4, align_bytes=64)
            copy = nc.vector.tensor_copy if (n, g) in COPY_ON_VECTOR else nc.scalar.copy
            copy(out=w_grouped[n, g][:], in_=w_raw[n, g][:].rearrange("p t n -> p n t"))

        def quantise(n, g):
            nc.vector.quantize_mx(
                out=w_code[n][:, g, :].bitcast(E4M3X4),
                scales=w_scale[n][:, g, :],
                in_=w_grouped[n, g][:].rearrange("p n t -> p (n t)"),
            )

        beta_f32 = keep.tile([P, P], F32, name="beta_f32")
        beta_column = keep.tile([P, H // P], F32, name="beta_column")
        beta_spread = keep.tile([P, BLOCK], F32, name="beta_spread")

        def turn_beta():
            nc.vector.tensor_copy(out=beta_f32[:], in_=beta_rows[:])
            bank = psum.tile([P, BLOCK], F32, name="turn")
            nc.tensor.transpose(bank[:, 0:P], beta_f32[:], identity[:])
            return bank

        def spread_beta():
            bank = psum.tile([P, BLOCK], F32, name="turn")
            first = QUARTERS * (HID_BLOCKS - 1)
            for s in range(QUARTERS):
                column = beta_column[:, first + s : first + s + 1].to_broadcast([P, P])
                nc.tensor.transpose(bank[:, P * s : P * (s + 1)], column, identity[:])
            nc.scalar.copy(out=beta_spread[:], in_=bank[:])

        acc = {}
        sums = {}
        turned = {}
        factor = {}

        def open_bank(k, s):
            acc[k, s] = psum.tile([P, BLOCK], F32, name="acc")

        def one_pass(k, s, g):
            n, c = STEPS[k]
            quarter = slice(P * s, P * (s + 1))
            w_side = (w_code[n][:, g, :], w_scale[n][:, g, :])
            g_side = (g_code[c][:, g, :], g_scale[:, g, BLOCK * c : BLOCK * (c + 1)])
            if k < LAST:
                (still, still_scale), still_type = w_side, E4M3X4
                (moving, moving_scale), moving_type = g_side, E5M2X4
            else:
                (still, still_scale), still_type = g_side, E5M2X4
                (moving, moving_scale), moving_type = w_side, E4M3X4
            nc.tensor.matmul_mx(
                out=acc[k, s][:],
                lhsT=still[:, quarter].bitcast(still_type),
                lhsT_scale=still_scale[:, quarter],
                rhs=moving.bitcast(moving_type),
                rhs_scale=moving_scale,
                start=(g == 0),
                stop=(g == PASSES - 1),
            )

        def multiply(k, s):
            open_bank(k, s)
            for g in range(PASSES):
                one_pass(k, s, g)

        def empty_with_beta(k, s):
            n, c = STEPS[k]
            sums[k, s] = work.tile([P, BLOCK], F32, name="sums", bufs=6)
            col = QUARTERS * n + s
            nc.scalar.activation(
                out=sums[k, s][:], in_=acc[k, s][:], func=IDENTITY, bias=beta_column[:, col : col + 1]
            )

        def turn(k):
            for e in range(QUARTERS):
                turned[k, e] = psum.tile([P, BLOCK], F32, name="turn")
                for s in range(QUARTERS):
                    nc.tensor.transpose(
                        turned[k, e][:, P * s : P * (s + 1)], sums[k, s][:, P * e : P * (e + 1)], identity[:]
                    )

        def make_factor(k, e):
            x = h_view[STEPS[k]][:, e, :]
            factor[k, e] = work.tile([P, BLOCK], F32, name="factor", bufs=12)
            nc.vector.scalar_tensor_tensor(out=factor[k, e][:], in0=x, scalar=1.0, in1=x, op0=SUB, op1=MULT)

        def scale_by_factor(out_tile, summed, k, e):
            nc.vector.scalar_tensor_tensor(
                out=out_tile, in0=summed[:], scalar=-1.0, in1=factor[k, e][:], op0=MULT, op1=MULT
            )

        def rows_of(k):
            n, c = STEPS[k]
            block = out[BLOCK * c : BLOCK * (c + 1), BLOCK * n : BLOCK * (n + 1)]
            return block.rearrange("(e p) n -> p e n", p=P)

        def finish(k, half):
            result = work.tile([P, 2, BLOCK], F32, name="result", bufs=8)
            for i in range(2):
                scale_by_factor(result[:, i, :], turned[k, 2 * half + i], k, 2 * half + i)
            nc.sync.dma_start(out=rows_of(k)[:, 2 * half : 2 * half + 2, :], in_=result[:])

        def side_work(t):
            for n in COPY_AT:
                for g in range(PASSES):
                    if COPY_AT[n][g] == t:
                        interleave(n, g)
                for g in range(PASSES):
                    if QUANTISE_AT[n][g] == t:
                        quantise(n, g)
            if t == SPREAD_BETA_AT:
                spread_beta()
            k, half = divmod(t, 2)
            for e in (2 * half, 2 * half + 1):
                make_factor(k, e)
            for e in range(QUARTERS):
                if LAST_FACTORS_AT[e] == t:
                    make_factor(LAST, e)

        interleave(0, 0)
        quantise(0, 0)
        interleave(0, 2)
        interleave(0, 1)
        beta_bank = turn_beta()
        quantise(0, 1)
        interleave(0, 3)
        nc.scalar.copy(out=beta_column[:], in_=beta_bank[:, 0 : H // P])
        quantise(0, 2)
        quantise(0, 3)

        for s in range(QUARTERS):
            open_bank(0, s)
        for g in range(PASSES):
            for s in range(QUARTERS):
                one_pass(0, s, g)
        for s in range(QUARTERS):
            empty_with_beta(0, s)
        side_work(0)
        side_work(1)

        for k in range(1, LAST):
            for half in range(2):
                for s in (2 * half, 2 * half + 1):
                    multiply(k, s)
                if half == 0:
                    turn(k - 1)
                for s in (2 * half, 2 * half + 1):
                    empty_with_beta(k, s)
                side_work(2 * k + half)
                finish(k - 1, half)

        with_beta = {}

        def add_beta(e):
            with_beta[e] = work.tile([P, BLOCK], F32, name="with_beta", bufs=4)
            nc.vector.tensor_tensor(out=with_beta[e][:], in0=acc[LAST, e][:], in1=beta_spread[:], op=ADD)

        def finish_last(e):
            result = work.tile([P, BLOCK], F32, name="result_last", bufs=4)
            scale_by_factor(result[:], with_beta[e], LAST, e)
            nc.sync.dma_start(out=rows_of(LAST)[:, e, :], in_=result[:])

        multiply(LAST, 0)
        turn(LAST - 1)
        finish(LAST - 1, 0)
        multiply(LAST, 1)
        finish(LAST - 1, 1)
        add_beta(0)
        add_beta(1)
        finish_last(0)
        for e in (2, 3):
            multiply(LAST, e)
            add_beta(e)
            finish_last(e - 1)
        finish_last(3)
